import numpy as np
import ml_dtypes


def mxq(x, axis, fmt="e4m3"):
    dtype, down = {"e4m3": (ml_dtypes.float8_e4m3fn, 7), "e5m2": (ml_dtypes.float8_e5m2, 14)}[fmt]
    v = np.moveaxis(np.asarray(x, np.float32).astype(ml_dtypes.bfloat16).astype(np.float64), axis, -1)
    blocks = v.reshape(v.shape[:-1] + (-1, 32))
    amax = np.abs(blocks).max(-1, keepdims=True)
    byte = np.maximum(np.where(amax > 0, np.frexp(amax)[1] - 1 + 127, 0) - down, 1)
    scale = np.exp2(byte - 127.0)
    codes = (blocks / scale).astype(np.float32).astype(dtype).astype(np.float64)
    return np.moveaxis((codes * scale).reshape(v.shape), -1, axis)


WIDE = False


def mx_kscale(k):
    if not WIDE:
        return np.ones(k)
    levels = np.array([10, -10, 5, -5, 0])
    if k % 512:
        return np.exp2(np.random.permutation(np.resize(levels, k // 32))).repeat(32)
    a = np.empty((k // 512, 16))
    for p in range(k // 512):
        a[p, :8] = np.random.permutation(np.resize(levels, 8))
        for g in range(8):
            far = levels[np.abs(levels - a[p, g]) >= 10]
            a[p, g + 8] = far[np.random.randint(len(far))]
    return np.exp2(a.ravel()).repeat(32)


def f64(x):
    return np.asarray(x).astype(np.float64)


def striped(idx):
    return np.tile(idx.reshape(-1, 16).T, (8, 1)).astype(np.uint16)


def unstriped(offs):
    return offs[:16].T.reshape(-1).astype(np.int64)


E2M1 = np.array([0.0, 0.5, 1.0, 1.5, 2.0, 3.0, 4.0, 6.0, -0.0, -0.5, -1.0, -1.5, -2.0, -3.0, -4.0, -6.0])


def pack_weight(w, fmt):
    k, n = w.shape
    w = f64(np.asarray(w, np.float32).astype(ml_dtypes.bfloat16)).reshape(k // 32, 32, n)
    amax = np.abs(w).max(1)
    if fmt == "e4m3":
        byte = np.frexp(amax)[1] - 1 + 127 - 7
    else:
        mant, ex = np.frexp(amax / 6.0)
        byte = np.where(mant > 0.5, ex, ex - 1) + 127
    byte = np.clip(np.where(amax > 0, byte, 1), 1, 254)
    scaled = (w * np.exp2(127.0 - byte)[:, None, :]).reshape(k, n).astype(np.float32)
    by_word = np.ascontiguousarray(scaled.reshape(k // 512, 128, 4, n).transpose(0, 1, 3, 2))
    if fmt == "e4m3":
        words = by_word.astype(ml_dtypes.float8_e4m3fn).view(np.uint8)
    else:
        c = by_word.astype(ml_dtypes.float4_e2m1fn).view(np.uint8) & 0xF
        words = (c[..., 0::2] | (c[..., 1::2] << 4)).reshape(k // 512, 128, 2 * n)
    return np.ascontiguousarray(words), np.ascontiguousarray(byte.astype(np.uint8).reshape(k // 512, 16, n))


def unpack_weight(words, scales, fmt):
    g, _, n = scales.shape
    words = np.ascontiguousarray(words).reshape(g, 128, n, -1)
    if fmt == "e4m3":
        vals = words.view(ml_dtypes.float8_e4m3fn).astype(np.float64)
    else:
        nib = np.empty((g, 128, n, 4), np.uint8)
        nib[..., 0::2] = words & 0xF
        nib[..., 1::2] = words >> 4
        vals = E2M1[nib]
    vals = vals * np.repeat(np.exp2(scales.astype(np.float64) - 127.0), 8, axis=1)[..., None]
    return vals.transpose(0, 1, 3, 2).reshape(g * 512, n)


def planes(y):
    n, m = y.shape
    v = y.astype(np.float32).astype(ml_dtypes.bfloat16).astype(np.float64).reshape(n // 32, 32, m)
    top = np.abs(v).max(1)
    byte = np.clip(np.where(top > 0, np.frexp(top)[1] - 1 + 127 - 7, 1), 1, 254)
    codes = (v * np.exp2(127.0 - byte)[:, None, :]).reshape(n, m).astype(np.float32).astype(ml_dtypes.float8_e4m3fn).view(np.uint8)
    words = codes.reshape(n // 512, 128, 4, m).transpose(0, 1, 3, 2)
    return np.ascontiguousarray(words), np.ascontiguousarray(byte.astype(np.uint8).reshape(n // 512, 16, m))


def relu(v):
    return np.maximum(v, 0.0)


K, T, E, C, H, TOP, COPIES = 512, 1024, 8, 128, 512, 2, 768
PAD = 64


def by_expert(wq, xq):
    return np.concatenate([wq[e].T @ xq[:, e * C:(e + 1) * C] for e in range(E)], axis=1)


def setup_inputs():
    n = np.random.standard_normal
    s = mx_kscale(K)
    u = mx_kscale(H)
    left = TOP * T - E * C - COPIES
    deal = np.repeat(np.arange(E + 2), [C] * E + [COPIES, left]).reshape(TOP, T)[:, np.random.permutation(T)]
    deal = np.take_along_axis(deal, np.argsort(np.random.rand(TOP, T), axis=0), axis=0)
    for _ in range(8):
        s_, t_ = np.random.permutation(T).reshape(2, -1); r = np.random.randint(TOP, size=T // 2); x, y = deal[r, s_].copy(), deal[r, t_].copy()
        ok = ~((deal[:, s_] == y).any(0) | (deal[:, t_] == x).any(0)); deal[r[ok], s_[ok]] = y[ok]; deal[r[ok], t_[ok]] = x[ok]
    order = np.lexsort((np.random.rand(TOP * T), deal.reshape(-1)))[:E * C]
    slot_token = order % T
    pos = np.where(deal == E, E * C + np.arange(T), E * C + T + np.arange(T) % PAD).reshape(-1); pos[order] = np.arange(E * C); pos = pos.reshape(TOP, T)
    g = np.random.uniform(0.5, 1.5, (TOP, T)); g = g / g.sum(0)
    xf = n((K, T))
    x = pack_weight(xf * s[:, None], "e4m3")
    w1 = [pack_weight(m, "e2m1") for m in n((E, K, H)) / np.sqrt(K) / s[None, :, None]]
    w3 = [pack_weight(m, "e2m1") for m in n((E, K, H)) / np.sqrt(K) / s[None, :, None] * u]
    w2 = [pack_weight(m, "e2m1") for m in n((E, H, K)) / np.sqrt(H) / u[None, :, None]]
    return {
        "x_words": x[0],
        "x_scales": x[1],
        "xr": (xf).astype(np.float32),
        "w1_words": np.stack([m[0] for m in w1]),
        "w1_scales": np.stack([m[1] for m in w1]),
        "w3_words": np.stack([m[0] for m in w3]),
        "w3_scales": np.stack([m[1] for m in w3]),
        "w2_words": np.stack([m[0] for m in w2]),
        "w2_scales": np.stack([m[1] for m in w2]),
        "gate": np.stack([np.tile(r, (128, 1)) for r in g]).astype(np.float32),
        "offs": striped(slot_token),
        "pos1": striped(pos[0]),
        "pos2": striped(pos[1]),
    }


def reference(x_words, x_scales, xr, w1_words, w1_scales, w3_words, w3_scales, w2_words, w2_scales, gate, offs, pos1, pos2):
    w1 = np.stack([unpack_weight(w1_words[e], w1_scales[e], "e2m1") for e in range(E)])
    w3 = np.stack([unpack_weight(w3_words[e], w3_scales[e], "e2m1") for e in range(E)])
    w2 = np.stack([unpack_weight(w2_words[e], w2_scales[e], "e2m1") for e in range(E)])
    idx = unstriped(offs)
    xq = unpack_weight(x_words, x_scales, "e4m3")[:, idx]
    h = relu(by_expert(w1, xq)) * by_expert(w3, xq)
    y = by_expert(w2, mxq(h, 0, "e4m3"))
    y = np.concatenate([y, f64(xr), np.zeros((K, PAD))], axis=1)
    out = sum(f64(gate[r, :1]) * y[:, unstriped(p)] for r, p in enumerate((pos1, pos2)))
    out_0 = out
    return (out_0,) + planes(out_0)

@@ -1,0 +1,292 @@
+from contextlib import ExitStack
+
+import concourse.mybir as mybir
+from concourse.masks import make_identity
+
+K, T, E, C, H, PAD = 512, 1024, 8, 128, 512, 64
+S = E * C
+WIN = S + T + PAD
+FLOPS = 3 * 2 * K * H * S
+
+F32 = mybir.dt.float32
+BF16 = mybir.dt.bfloat16
+I32 = mybir.dt.int32
+U32 = mybir.dt.uint32
+U16 = mybir.dt.uint16
+U8 = mybir.dt.uint8
+FP8X4 = mybir.dt.float8_e4m3fn_x4
+FP4X4 = mybir.dt.float4_e2m1fn_x4
+ACT = mybir.ActivationFunctionType
+ALU = mybir.AluOpType
+
+P = 128
+NB = T // P
+CHUNKS = ((0, 3), (3, 3), (6, 2))
+MIN_OFFS = 288
+W_LOADS = ((0, 2), (2, 3), (5, 3))
+GROUPS = ((0, 2), (2, 2), (4, 2), (6, 1), (7, 1))
+
+
+def tile_moe_cpy_glu_relu_kernel(
+    tc, x_words, x_scales, xr, w1_words, w1_scales, w3_words, w3_scales, w2_words, w2_scales,
+    gate, offs, pos1, pos2, out_0, out_1, out_2,
+):
+    nc = tc.nc
+    with ExitStack() as ctx:
+        keep = ctx.enter_context(tc.tile_pool(name="keep", bufs=1))
+        ring = ctx.enter_context(tc.tile_pool(name="ring", bufs=2))
+        psum = ctx.enter_context(tc.psum_pool(name="psum", bufs=1))
+
+        def bank(b, shape, name):
+            return psum.tile(shape, F32, name=name, tag="bank%d" % b)
+
+        def held(shape, dtype, name):
+            return keep.tile(shape, dtype, name=name, align_bytes=64)
+
+        offs_t = keep.tile([P, S // 16], U16, name="offs_t")
+        pos_t = [keep.tile([P, T // 16], U16, name="pos%d_t" % r) for r in (1, 2)]
+        xw = held([P, T], I32, "xw")
+        xs = held([P, T], U8, "xs")
+        w1s = held([P, E * H], U8, "w1s")
+        w3s = held([P, E * H], U8, "w3s")
+        w2s = held([P, E * K], U8, "w2s")
+        w1w = [held([P, n * 2 * H], U8, "w1w%d" % e0) for e0, n in W_LOADS]
+        w3w = [held([P, n * 2 * H], U8, "w3w%d" % e0) for e0, n in W_LOADS]
+        w2first = held([P, E, 256], U8, "w2first")
+        w2rest = held([P, E, 768], U8, "w2rest")
+        win = [held([P, WIN], F32, "win%d" % j) for j in range(4)]
+        ident = held([P, P], F32, "ident")
+        grows = held([P, P], F32, "grows")
+        gcol = held([P, 2 * NB], F32, "gcol")
+
+        def load_scales(plane, src, n_e):
+            view = src.rearrange("e s (q r) w -> r q (e s) w", r=4)
+            dst = plane[:].rearrange("p (e w) -> p e w", e=n_e)
+            for r in range(4):
+                nc.sync.dma_start(out=dst[r:P:32].bitcast(I32), in_=view[r].bitcast(I32))
+
+        def load_words(dst, src, i):
+            e0, n = W_LOADS[i]
+            view = src.rearrange("e s p c -> p (e s) c")[:, e0:e0 + n, :]
+            nc.sync.dma_start(out=dst[i][:].rearrange("p (e c) -> p e c", e=n).bitcast(I32), in_=view.bitcast(I32))
+
+        def expert_words(tiles, e):
+            i = max(k for k, (e0, n) in enumerate(W_LOADS) if e0 <= e)
+            u = e - W_LOADS[i][0]
+            return tiles[i][:, u * 2 * H:(u + 1) * 2 * H]
+
+        nc.vector.memset(xs[:].bitcast(I32), 0)
+        nc.vector.memset(w1s[:].bitcast(I32), 0)
+        nc.vector.memset(w3s[:].bitcast(I32), 0)
+        nc.vector.memset(w2s[:].bitcast(I32), 0)
+        for j in range(4):
+            nc.vector.memset(win[j][:, S + T:], 0.0)
+        nc.gpsimd.memset(grows[:], 0.0)
+        gate_rows = gate.rearrange("r a (b c) -> (r a b) c", c=P)
+        nc.gpsimd.dma_start(out=grows[0:2 * NB, :], in_=gate_rows[(P - 1) * NB:(P + 1) * NB, :])
+        make_identity(nc, ident[:])
+
+        nc.sync.dma_start(offs_t[:], offs)
+        nc.sync.dma_start(out=xw[:], in_=x_words.rearrange("s p t d -> p (s t d)").bitcast(I32))
+        xs_view = x_scales.rearrange("s (q r) t -> r q (s t)", r=4)
+        for r in range(4):
+            nc.sync.dma_start(out=xs[r:P:32, :].bitcast(I32), in_=xs_view[r].bitcast(I32))
+        load_words(w1w, w1_words, 0)
+        load_words(w3w, w3_words, 0)
+        load_scales(w1s, w1_scales, E)
+        load_scales(w3s, w3_scales, E)
+        for i in (1, 2):
+            load_words(w1w, w1_words, i)
+            load_words(w3w, w3_words, i)
+        load_scales(w2s, w2_scales, E)
+        w2_view = w2_words.rearrange("e s p c -> p (e s) c")
+        nc.sync.dma_start(out=w2first[:].bitcast(I32), in_=w2_view[:, :, 0:256].bitcast(I32))
+        nc.sync.dma_start(out=win[0][:, S:S + T], in_=xr[0:P, :])
+        nc.sync.dma_start(pos_t[0][:], pos1)
+        nc.sync.dma_start(pos_t[1][:], pos2)
+        nc.sync.dma_start(out=w2rest[:].bitcast(I32), in_=w2_view[:, :, 256:1024].bitcast(I32))
+        for j in range(1, 4):
+            nc.sync.dma_start(out=win[j][:, S:S + T], in_=xr[j * P:(j + 1) * P, :])
+
+        gps = bank(5, [P, P], "gps")
+        nc.tensor.transpose(gps[:], grows[:], ident[:])
+        nc.scalar.activation(gcol[:], gps[:, 0:2 * NB], ACT.Copy)
+
+        xg, xgs = [], []
+
+        def gather_tokens(pr):
+            gw = ring.tile([P, 2 * C], I32, name="xg", bufs=3, align_bytes=64)
+            gs = ring.tile([P, 2 * C], U8, name="xgs", bufs=3, align_bytes=64)
+            sl = offs_t[:, pr * 16:(pr + 1) * 16]
+            nc.vector.tensor_copy(gw[:].bitcast(U32), xw[:].bitcast(U32).indirect(sl))
+            nc.vector.tensor_copy(gs[:], xs[:].indirect(sl))
+            xg.append(gw)
+            xgs.append(gs)
+
+        hq, hqs = {}, {}
+
+        def w2_cols(e, j):
+            if j == 0:
+                return w2first[:, e, :]
+            return w2rest[:, e, (j - 1) * 256:j * 256]
+
+        def second_layer(dst, j, e):
+            nc.tensor.matmul_mx(
+                out=dst, lhsT=w2_cols(e, j).bitcast(FP4X4),
+                lhsT_scale=w2s[:, e * K + j * P:e * K + (j + 1) * P],
+                rhs=hq[e].bitcast(FP8X4), rhs_scale=hqs[e], start=True, stop=True,
+            )
+
+        hb = {}
+
+        def first_layer(e):
+            pr, u = divmod(e, 2)
+            tok = xg[pr][:, u * C:(u + 1) * C].bitcast(FP8X4)
+            tok_s = xgs[pr][:, u * C:(u + 1) * C]
+            a = bank(e % 3, [P, H], "a")
+            b = bank((3, 4, 6, 7)[e % 4], [P, H], "b")
+            for dst, ww, ws in ((a, w1w, w1s), (b, w3w, w3s)):
+                nc.tensor.matmul_mx(
+                    out=dst[:], lhsT=tok, lhsT_scale=tok_s,
+                    rhs=expert_words(ww, e).bitcast(FP4X4),
+                    rhs_scale=ws[:, e * H:(e + 1) * H], start=True, stop=True,
+                )
+            ra = ring.tile([P, H], F32, name="ra", bufs=4)
+            nc.scalar.activation(
+                ra[:].rearrange("s (u p w) -> s u p w", u=2, w=2),
+                a[:].rearrange("s (p u w) -> s u p w", u=2, w=2), ACT.Relu)
+            h = ring.tile([P, H], BF16, name="h", bufs=4, align_bytes=64)
+            nc.vector.tensor_tensor(
+                h[:].rearrange("s (u p w) -> s u p w", u=2, w=2),
+                b[:].rearrange("s (p u w) -> s u p w", u=2, w=2),
+                ra[:].rearrange("s (u p w) -> s u p w", u=2, w=2), ALU.mult)
+            hb[e] = h
+
+        def turn_and_quantise(gi, bk):
+            e0, n = GROUPS[gi]
+            ht = bank(bk, [P, n, 2, C], "ht")
+            for u in range(n):
+                words = hb[e0 + u][:].bitcast(F32)
+                for v in range(2):
+                    nc.tensor.transpose(ht[:, u, v, :], words[:, v * P:(v + 1) * P], ident[:])
+            hin = ring.tile([P, n * H], BF16, name="hin", align_bytes=64)
+            nc.scalar.copy(
+                hin[:].bitcast(F32).rearrange("p (u s v) -> p u s v", u=n, v=2),
+                ht[:].rearrange("p u v s -> p u s v"))
+            q = held([P, n * C], U32, "hq%d" % gi)
+            qs = held([P, n * C], U8, "hqs%d" % gi)
+            nc.vector.quantize_mx(out=q[:].bitcast(FP8X4), scales=qs[:], in_=hin[:])
+            for u in range(n):
+                hq[e0 + u] = q[:, u * C:(u + 1) * C]
+                hqs[e0 + u] = qs[:, u * C:(u + 1) * C]
+
+        def slots_out(j, e0, n, bk):
+            yb = bank(bk, [P, n * C], "y")
+            for u in range(n):
+                second_layer(yb[:, u * C:(u + 1) * C], j, e0 + u)
+            nc.scalar.copy(win[j][:, e0 * C:(e0 + n) * C], yb[:])
+
+        for pr in range(3):
+            gather_tokens(pr)
+        first_layer(0)
+        first_layer(1)
+        gather_tokens(3)
+        first_layer(2)
+        first_layer(3)
+        turn_and_quantise(0, 5)
+        first_layer(4)
+        first_layer(5)
+        turn_and_quantise(1, 5)
+        first_layer(6)
+        first_layer(7)
+        turn_and_quantise(2, 5)
+        slots_out(0, 0, 4, 2)
+        turn_and_quantise(3, 3)
+        turn_and_quantise(4, 5)
+        slots_out(0, 4, 3, 0)
+        slots_out(0, 7, 1, 4)
+
+        def row_block(j, banks):
+            for hf in range(2):
+                slots_out(j, 4 * hf, 4, banks[hf])
+
+        row_block(1, (1, 6))
+        row_block(2, (7, 3))
+
+        sc = [[held([P, 4, P], F32, "sc%d_%d" % (r, tb)) for tb in range(NB)] for r in range(2)]
+
+        def scale_out(r, tb, src, j0, nj):
+            nc.scalar.activation(
+                sc[r][tb][:, :, 32 * j0:32 * (j0 + nj)],
+                src.rearrange("c (p d) -> c d p", d=4),
+                ACT.Copy, scale=gcol[:, r * NB + tb:r * NB + tb + 1])
+
+        for r in range(2):
+            g = ring.tile([P, T], F32, name="g0", tag="g0")
+            nc.vector.tensor_copy(g[:], win[0][:].indirect(pos_t[r][:]))
+            for hf in range(2):
+                fb = bank(((5, 2), (0, 4))[r][hf], [P, 4, P], "fb0")
+                for i in range(4):
+                    tb = 4 * hf + i
+                    nc.tensor.transpose(fb[:, i, :], g[:, tb * P:(tb + 1) * P], ident[:])
+                for i in range(4):
+                    scale_out(r, 4 * hf + i, fb[:, i, :], 0, 1)
+            if r == 0:
+                row_block(3, (1, 6))
+
+        codes = held([P, T], U32, "codes")
+        planes = held([P, T], U8, "planes")
+        out_rows = out_0.rearrange("(p d) t -> p d t", d=4)
+        out_words = out_1.rearrange("s p t d -> p (s t d)").bitcast(I32)
+        out_scales = out_2.rearrange("s (q r) t -> r q (s t)", r=4)
+
+        def forward(r, tb0, ntb, banks):
+            n = max(ntb * P, MIN_OFFS)
+            first = (tb0 + ntb) * P - n
+            skip = n - ntb * P
+            fbs = [bank(banks[i], [P, 3 * P], "fb") for i in range(ntb)]
+            for j in range(1, 4):
+                g = ring.tile([P, 3 * P], F32, name="g", bufs=18)
+                nc.vector.tensor_copy(g[:, 0:n], win[j][:].indirect(pos_t[r][:, first // 16:(first + n) // 16]))
+                for i in range(ntb):
+                    nc.tensor.transpose(fbs[i][:, (j - 1) * P:j * P], g[:, skip + i * P:skip + (i + 1) * P], ident[:])
+            for i in range(ntb):
+                scale_out(r, tb0 + i, fbs[i][:], 1, 3)
+
+        osb = {}
+
+        def backward(tb0, ntb):
+            osb[tb0] = held([P, 4, ntb * P], F32, "osb%d" % tb0)
+            for i in range(ntb):
+                tb = tb0 + i
+                ob = bank((1, 6)[tb % 2], [P, 4, P], "ob")
+                for d in range(4):
+                    for r in range(2):
+                        nc.tensor.matmul(ob[:, d, :], sc[r][tb][:, d, :], ident[:], is_transpose=True,
+                                         start=(r == 0), stop=(r == 1))
+                nc.scalar.copy(osb[tb0][:, :, i * P:(i + 1) * P], ob[:])
+            nc.sync.dma_start(out=out_rows[:, :, tb0 * P:(tb0 + ntb) * P], in_=osb[tb0][:])
+
+        def planes_of(tb0, pieces):
+            i = 0
+            for n in pieces:
+                rb = ring.tile([P, 4 * n * P], BF16, name="rb", bufs=6, align_bytes=64)
+                nc.vector.tensor_copy(rb[:].rearrange("p (c d) -> p c d", d=4),
+                                      osb[tb0][:, :, i * P:(i + n) * P].rearrange("p d c -> p c d"))
+                cols = slice((tb0 + i) * P, (tb0 + i + n) * P)
+                nc.vector.quantize_mx(out=codes[:, cols].bitcast(FP8X4), scales=planes[:, cols], in_=rb[:])
+                i = i + n
+            cols = slice(tb0 * P, (tb0 + i) * P)
+            nc.sync.dma_start(out=out_words[:, cols], in_=codes[:, cols].bitcast(I32))
+
+        for ci, (tb0, ntb) in enumerate(CHUNKS):
+            forward(0, tb0, ntb, (7, 3, 5))
+            if ci > 0:
+                backward(*CHUNKS[ci - 1])
+            forward(1, tb0, ntb, (2, 0, 4))
+        backward(*CHUNKS[-1])
+        planes_of(0, (2, 1))
+        planes_of(3, (2, 1))
+        planes_of(6, (1, 1))
+        for r in range(4):
+            nc.sync.dma_start(out=out_scales[r].bitcast(I32), in_=planes[r:P:32, :].bitcast(I32))

@@ -21,8 +21,9 @@ ALU = mybir.AluOpType
 
 P = 128
 NB = T // P
-CHUNKS = ((0, 3), (3, 3), (6, 2))
-MIN_OFFS = 288
+GB = 5
+KICKS = (0, 0, 0)
+LATE_Y3 = False
 W_LOADS = ((0, 2), (2, 3), (5, 3))
 GROUPS = ((0, 2), (2, 2), (4, 2), (6, 1), (7, 1))
 
@@ -52,8 +53,7 @@ def tile_moe_cpy_glu_relu_kernel(
         w2s = held([P, E * K], U8, "w2s")
         w1w = [held([P, n * 2 * H], U8, "w1w%d" % e0) for e0, n in W_LOADS]
         w3w = [held([P, n * 2 * H], U8, "w3w%d" % e0) for e0, n in W_LOADS]
-        w2first = held([P, E, 256], U8, "w2first")
-        w2rest = held([P, E, 768], U8, "w2rest")
+        w2w = [held([P, E, 512], U8, "w2w%d" % jp) for jp in range(2)]
         win = [held([P, WIN], F32, "win%d" % j) for j in range(4)]
         ident = held([P, P], F32, "ident")
         grows = held([P, P], F32, "grows")
@@ -75,21 +75,22 @@ def tile_moe_cpy_glu_relu_kernel(
             u = e - W_LOADS[i][0]
             return tiles[i][:, u * 2 * H:(u + 1) * 2 * H]
 
-        nc.vector.memset(xs[:].bitcast(I32), 0)
+        nc.gpsimd.memset(xs[:].bitcast(I32), 0)
         nc.vector.memset(w1s[:].bitcast(I32), 0)
         nc.vector.memset(w3s[:].bitcast(I32), 0)
-        nc.vector.memset(w2s[:].bitcast(I32), 0)
-        for j in range(4):
-            nc.vector.memset(win[j][:, S + T:], 0.0)
         nc.gpsimd.memset(grows[:], 0.0)
         gate_rows = gate.rearrange("r a (b c) -> (r a b) c", c=P)
         nc.gpsimd.dma_start(out=grows[0:2 * NB, :], in_=gate_rows[(P - 1) * NB:(P + 1) * NB, :])
         make_identity(nc, ident[:])
+        nc.gpsimd.memset(w2s[:].bitcast(I32), 0)
+        for j in range(4):
+            nc.gpsimd.memset(win[j][:, S + T:], 0.0)
 
         nc.sync.dma_start(offs_t[:], offs)
-        nc.sync.dma_start(out=xw[:], in_=x_words.rearrange("s p t d -> p (s t d)").bitcast(I32))
         xs_view = x_scales.rearrange("s (q r) t -> r q (s t)", r=4)
         for r in range(4):
+            if r == 3:
+                nc.sync.dma_start(out=xw[:], in_=x_words.rearrange("s p t d -> p (s t d)").bitcast(I32))
             nc.sync.dma_start(out=xs[r:P:32, :].bitcast(I32), in_=xs_view[r].bitcast(I32))
         load_words(w1w, w1_words, 0)
         load_words(w3w, w3_words, 0)
@@ -100,24 +101,31 @@ def tile_moe_cpy_glu_relu_kernel(
             load_words(w3w, w3_words, i)
         load_scales(w2s, w2_scales, E)
         w2_view = w2_words.rearrange("e s p c -> p (e s) c")
-        nc.sync.dma_start(out=w2first[:].bitcast(I32), in_=w2_view[:, :, 0:256].bitcast(I32))
-        nc.sync.dma_start(out=win[0][:, S:S + T], in_=xr[0:P, :])
-        nc.sync.dma_start(pos_t[0][:], pos1)
-        nc.sync.dma_start(pos_t[1][:], pos2)
-        nc.sync.dma_start(out=w2rest[:].bitcast(I32), in_=w2_view[:, :, 256:1024].bitcast(I32))
-        for j in range(1, 4):
+        def load_w2(jp):
+            nc.sync.dma_start(out=w2w[jp][:].bitcast(I32), in_=w2_view[:, :, 512 * jp:512 * (jp + 1)].bitcast(I32))
+
+        def load_xr(j):
             nc.sync.dma_start(out=win[j][:, S:S + T], in_=xr[j * P:(j + 1) * P, :])
 
-        gps = bank(5, [P, P], "gps")
+        load_w2(0)
+        load_xr(0)
+        load_xr(1)
+        load_w2(1)
+        nc.sync.dma_start(pos_t[0][:], pos1)
+        load_xr(2)
+        load_xr(3)
+        nc.sync.dma_start(pos_t[1][:], pos2)
+
+        gps = bank(7, [P, P], "gps")
         nc.tensor.transpose(gps[:], grows[:], ident[:])
         nc.scalar.activation(gcol[:], gps[:, 0:2 * NB], ACT.Copy)
 
         xg, xgs = [], []
 
-        def gather_tokens(pr):
-            gw = ring.tile([P, 2 * C], I32, name="xg", bufs=3, align_bytes=64)
-            gs = ring.tile([P, 2 * C], U8, name="xgs", bufs=3, align_bytes=64)
-            sl = offs_t[:, pr * 16:(pr + 1) * 16]
+        for hf in range(2):
+            gw = held([P, 4 * C], I32, "xg%d" % hf)
+            gs = held([P, 4 * C], U8, "xgs%d" % hf)
+            sl = offs_t[:, hf * 32:(hf + 1) * 32]
             nc.vector.tensor_copy(gw[:].bitcast(U32), xw[:].bitcast(U32).indirect(sl))
             nc.vector.tensor_copy(gs[:], xs[:].indirect(sl))
             xg.append(gw)
@@ -126,9 +134,7 @@ def tile_moe_cpy_glu_relu_kernel(
         hq, hqs = {}, {}
 
         def w2_cols(e, j):
-            if j == 0:
-                return w2first[:, e, :]
-            return w2rest[:, e, (j - 1) * 256:j * 256]
+            return w2w[j // 2][:, e, (j % 2) * 256:(j % 2 + 1) * 256]
 
         def second_layer(dst, j, e):
             nc.tensor.matmul_mx(
@@ -140,10 +146,10 @@ def tile_moe_cpy_glu_relu_kernel(
         hb = {}
 
         def first_layer(e):
-            pr, u = divmod(e, 2)
+            pr, u = divmod(e, 4)
             tok = xg[pr][:, u * C:(u + 1) * C].bitcast(FP8X4)
             tok_s = xgs[pr][:, u * C:(u + 1) * C]
-            a = bank(e % 3, [P, H], "a")
+            a = bank((0, 1, 2, 5)[e % 4], [P, H], "a")
             b = bank((3, 4, 6, 7)[e % 4], [P, H], "b")
             for dst, ww, ws in ((a, w1w, w1s), (b, w3w, w3s)):
                 nc.tensor.matmul_mx(
@@ -155,7 +161,7 @@ def tile_moe_cpy_glu_relu_kernel(
             nc.scalar.activation(
                 ra[:].rearrange("s (u p w) -> s u p w", u=2, w=2),
                 a[:].rearrange("s (p u w) -> s u p w", u=2, w=2), ACT.Relu)
-            h = ring.tile([P, H], BF16, name="h", bufs=4, align_bytes=64)
+            h = ring.tile([P, H], BF16, name="h", bufs=8, align_bytes=64)
             nc.vector.tensor_tensor(
                 h[:].rearrange("s (u p w) -> s u p w", u=2, w=2),
                 b[:].rearrange("s (p u w) -> s u p w", u=2, w=2),
@@ -169,8 +175,9 @@ def tile_moe_cpy_glu_relu_kernel(
                 words = hb[e0 + u][:].bitcast(F32)
                 for v in range(2):
                     nc.tensor.transpose(ht[:, u, v, :], words[:, v * P:(v + 1) * P], ident[:])
-            hin = ring.tile([P, n * H], BF16, name="hin", align_bytes=64)
-            nc.scalar.copy(
+            hin = ring.tile([P, n * H], BF16, name="hin", bufs=3, align_bytes=64)
+            copy = nc.scalar.copy if gi < 2 else nc.vector.tensor_copy
+            copy(
                 hin[:].bitcast(F32).rearrange("p (u s v) -> p u s v", u=n, v=2),
                 ht[:].rearrange("p u v s -> p u s v"))
             q = held([P, n * C], U32, "hq%d" % gi)
@@ -186,107 +193,149 @@ def tile_moe_cpy_glu_relu_kernel(
                 second_layer(yb[:, u * C:(u + 1) * C], j, e0 + u)
             nc.scalar.copy(win[j][:, e0 * C:(e0 + n) * C], yb[:])
 
-        for pr in range(3):
-            gather_tokens(pr)
-        first_layer(0)
-        first_layer(1)
-        gather_tokens(3)
-        first_layer(2)
-        first_layer(3)
-        turn_and_quantise(0, 5)
-        first_layer(4)
-        first_layer(5)
-        turn_and_quantise(1, 5)
-        first_layer(6)
-        first_layer(7)
-        turn_and_quantise(2, 5)
-        slots_out(0, 0, 4, 2)
-        turn_and_quantise(3, 3)
-        turn_and_quantise(4, 5)
-        slots_out(0, 4, 3, 0)
-        slots_out(0, 7, 1, 4)
-
+        for e in range(E):
+            first_layer(e)
+        for gi, bk in enumerate((0, 1, 2, 5, 3)):
+            turn_and_quantise(gi, bk)
+        slots_out(0, 0, 4, 4)
+        slots_out(0, 4, 3, 6)
+        slots_out(0, 7, 1, 7)
+        slots_out(1, 0, 4, 0)
+        slots_out(1, 4, 3, 1)
+        slots_out(1, 7, 1, 2)
+        A, B, Cb, D, Eb, Fb, G, Hb = 0, 1, 2, 5, 3, 4, 6, 7
         def row_block(j, banks):
             for hf in range(2):
                 slots_out(j, 4 * hf, 4, banks[hf])
 
-        row_block(1, (1, 6))
-        row_block(2, (7, 3))
+        def kick(n, bk):
+            if n:
+                spare = bank(bk, [P, H], "spare")
+            for i in range(n):
+                nc.tensor.matmul_mx(
+                    out=spare[:], lhsT=xg[0][:, 0:C].bitcast(FP8X4), lhsT_scale=xgs[0][:, 0:C],
+                    rhs=expert_words(w1w, 0).bitcast(FP4X4), rhs_scale=w1s[:, 0:H], start=True, stop=True)
 
-        sc = [[held([P, 4, P], F32, "sc%d_%d" % (r, tb)) for tb in range(NB)] for r in range(2)]
+        row_block(2, (D, Cb))
+        if not LATE_Y3:
+            row_block(3, (Eb, Fb))
 
-        def scale_out(r, tb, src, j0, nj):
-            nc.scalar.activation(
-                sc[r][tb][:, :, 32 * j0:32 * (j0 + nj)],
-                src.rearrange("c (p d) -> c d p", d=4),
-                ACT.Copy, scale=gcol[:, r * NB + tb:r * NB + tb + 1])
+        def place(jp, tb):
+            if jp == 0:
+                return tb % 4, tb // 4
+            return 2 * (tb // 4) + tb % 2, (tb % 4) // 2
 
-        for r in range(2):
-            g = ring.tile([P, T], F32, name="g0", tag="g0")
-            nc.vector.tensor_copy(g[:], win[0][:].indirect(pos_t[r][:]))
-            for hf in range(2):
-                fb = bank(((5, 2), (0, 4))[r][hf], [P, 4, P], "fb0")
-                for i in range(4):
-                    tb = 4 * hf + i
-                    nc.tensor.transpose(fb[:, i, :], g[:, tb * P:(tb + 1) * P], ident[:])
-                for i in range(4):
-                    scale_out(r, 4 * hf + i, fb[:, i, :], 0, 1)
+        sc = [[[held([P, 4, P], F32, "sc%d_%d_%d" % (r, jp, u)) for u in range(4)] for jp in range(2)]
+              for r in range(2)]
+        back = {}
+
+        def fetch(r, j, tb0, order, banks):
+            jp, jj = divmod(j, 2)
+            ntb = len(order)
+            g = ring.tile([P, ntb * P], F32, name="g", bufs=GB)
+            nc.vector.tensor_copy(g[:], win[j][:].indirect(pos_t[r][:, tb0 * 8:(tb0 + ntb) * 8]))
+            for k, bk in enumerate(banks):
+                fb = bank(bk, [P, 4, P], "fwd")
+                tbs = order[4 * k:4 * k + 4]
+                for i, tb in enumerate(tbs):
+                    nc.tensor.transpose(fb[:, i, :], g[:, (tb - tb0) * P:(tb - tb0 + 1) * P], ident[:])
+                for i, tb in enumerate(tbs):
+                    u, side = place(jp, tb)
+                    nc.scalar.activation(
+                        sc[r][jp][u][:, :, 64 * side + 32 * jj:64 * side + 32 * (jj + 1)],
+                        fb[:, i, :].rearrange("c (p d) -> c d p", d=4),
+                        ACT.Copy, scale=gcol[:, r * NB + tb:r * NB + tb + 1])
+
+        def turn_back(r, jp, u, bk):
             if r == 0:
-                row_block(3, (1, 6))
+                back[u] = bank(bk, [P, 4, P], "back")
+            for d in range(4):
+                nc.tensor.matmul(back[u][:, d, :], sc[r][jp][u][:, d, :], ident[:], is_transpose=True,
+                                 start=(r == 0 and d == 0), stop=(r == 1 and d == 3))
 
-        codes = held([P, T], U32, "codes")
-        planes = held([P, T], U8, "planes")
         out_rows = out_0.rearrange("(p d) t -> p d t", d=4)
         out_words = out_1.rearrange("s p t d -> p (s t d)").bitcast(I32)
-        out_scales = out_2.rearrange("s (q r) t -> r q (s t)", r=4)
+        out_scales = out_2.rearrange("s b t -> b (s t)").bitcast(I32)
+        osb0 = held([P, 4, 4 * P], F32, "osb0")
+        osb1 = [held([P, 4, 2 * P], F32, "osb1_%d" % h) for h in range(2)]
+        codes = [held([P, 4 * P], U32, "codes%d" % jp) for jp in range(2)]
+        planes = [held([P, 4 * P], U8, "planes%d" % jp) for jp in range(2)]
 
-        def forward(r, tb0, ntb, banks):
-            n = max(ntb * P, MIN_OFFS)
-            first = (tb0 + ntb) * P - n
-            skip = n - ntb * P
-            fbs = [bank(banks[i], [P, 3 * P], "fb") for i in range(ntb)]
-            for j in range(1, 4):
-                g = ring.tile([P, 3 * P], F32, name="g", bufs=18)
-                nc.vector.tensor_copy(g[:, 0:n], win[j][:].indirect(pos_t[r][:, first // 16:(first + n) // 16]))
-                for i in range(ntb):
-                    nc.tensor.transpose(fbs[i][:, (j - 1) * P:j * P], g[:, skip + i * P:skip + (i + 1) * P], ident[:])
-            for i in range(ntb):
-                scale_out(r, tb0 + i, fbs[i][:], 1, 3)
+        def sums(jp, u):
+            if jp == 0:
+                return osb0[:, :, u * P:(u + 1) * P]
+            return osb1[u // 2][:, :, (u % 2) * P:(u % 2 + 1) * P]
 
-        osb = {}
+        def round_out(jp, u0, n, src):
+            rb = rounded[:, (4 * jp + u0) * 4 * P:(4 * jp + u0 + n) * 4 * P]
+            nc.vector.tensor_copy(rb.rearrange("p (c d) -> p c d", d=4), src.rearrange("p d c -> p c d"))
 
-        def backward(tb0, ntb):
-            osb[tb0] = held([P, 4, ntb * P], F32, "osb%d" % tb0)
-            for i in range(ntb):
-                tb = tb0 + i
-                ob = bank((1, 6)[tb % 2], [P, 4, P], "ob")
-                for d in range(4):
-                    for r in range(2):
-                        nc.tensor.matmul(ob[:, d, :], sc[r][tb][:, d, :], ident[:], is_transpose=True,
-                                         start=(r == 0), stop=(r == 1))
-                nc.scalar.copy(osb[tb0][:, :, i * P:(i + 1) * P], ob[:])
-            nc.sync.dma_start(out=out_rows[:, :, tb0 * P:(tb0 + ntb) * P], in_=osb[tb0][:])
+        def quantise_out(jp, u0, n):
+            rb = rounded[:, (4 * jp + u0) * 4 * P:(4 * jp + u0 + n) * 4 * P]
+            cols = slice(u0 * P, (u0 + n) * P)
+            nc.vector.quantize_mx(out=codes[jp][:, cols].bitcast(FP8X4), scales=planes[jp][:, cols], in_=rb)
 
-        def planes_of(tb0, pieces):
-            i = 0
-            for n in pieces:
-                rb = ring.tile([P, 4 * n * P], BF16, name="rb", bufs=6, align_bytes=64)
-                nc.vector.tensor_copy(rb[:].rearrange("p (c d) -> p c d", d=4),
-                                      osb[tb0][:, :, i * P:(i + n) * P].rearrange("p d c -> p c d"))
-                cols = slice((tb0 + i) * P, (tb0 + i + n) * P)
-                nc.vector.quantize_mx(out=codes[:, cols].bitcast(FP8X4), scales=planes[:, cols], in_=rb[:])
-                i = i + n
-            cols = slice(tb0 * P, (tb0 + i) * P)
-            nc.sync.dma_start(out=out_words[:, cols], in_=codes[:, cols].bitcast(I32))
-
-        for ci, (tb0, ntb) in enumerate(CHUNKS):
-            forward(0, tb0, ntb, (7, 3, 5))
-            if ci > 0:
-                backward(*CHUNKS[ci - 1])
-            forward(1, tb0, ntb, (2, 0, 4))
-        backward(*CHUNKS[-1])
-        planes_of(0, (2, 1))
-        planes_of(3, (2, 1))
-        planes_of(6, (1, 1))
-        for r in range(4):
-            nc.sync.dma_start(out=out_scales[r].bitcast(I32), in_=planes[r:P:32, :].bitcast(I32))
+        order0 = (0, 4, 1, 5, 2, 6, 3, 7)
+        order1 = (0, 2, 1, 3, 4, 6, 5, 7)
+        fetch(0, 0, 0, order0, (G, Hb))
+        fetch(0, 1, 0, order0, (A, B))
+        turn_back(0, 0, 0, Cb)
+        turn_back(0, 0, 1, D)
+        fetch(1, 0, 0, order0, (A, B))
+        turn_back(0, 0, 2, Eb)
+        turn_back(0, 0, 3, Fb)
+        fetch(1, 1, 0, order0, (A, B))
+        for u in range(4):
+            if u == 2:
+                fetch(0, 2, 0, order1, (A, B))
+            turn_back(1, 0, u, None)
+            nc.scalar.copy(sums(0, u), back[u][:])
+        for side in range(2):
+            nc.sync.dma_start(out=out_rows[0:64, :, 512 * side:512 * (side + 1)], in_=osb0[64 * side:64 * (side + 1)])
+        fetch(0, 3, 0, order1, (Cb, D))
+        fetch(1, 2, 0, order1[0:4], (A,))
+        fetch(1, 3, 0, order1[0:4], (B,))
+        turn_back(0, 1, 0, G)
+        turn_back(0, 1, 1, Hb)
+        fetch(1, 2, 4, order1[4:8], (Cb,))
+        turn_back(0, 1, 2, Eb)
+        turn_back(0, 1, 3, Fb)
+        fetch(1, 3, 4, order1[4:8], (D,))
+        for u in range(4):
+            turn_back(1, 1, u, None)
+        rounded = keep.tile([P, 8 * 4 * P], BF16, name="rounded", tag="win3", align_bytes=64)
+        for h in range(2):
+            for u in (2 * h, 2 * h + 1):
+                nc.scalar.copy(sums(1, u), back[u][:])
+            for side in range(2):
+                first = 512 * h + 256 * side
+                nc.sync.dma_start(out=out_rows[64:P, :, first:first + 256], in_=osb1[h][64 * side:64 * (side + 1)])
+        for jp in range(2):
+            if jp == 0:
+                round_out(0, 0, 4, osb0[:])
+                quantise_out(0, 0, 4)
+            else:
+                round_out(1, 0, 2, osb1[0][:])
+                round_out(1, 2, 1, sums(1, 2))
+                quantise_out(1, 0, 2)
+                round_out(1, 3, 1, sums(1, 3))
+                quantise_out(1, 2, 1)
+                quantise_out(1, 3, 1)
+            for side in range(2):
+                rows = slice(64 * side, 64 * (side + 1))
+                if jp == 0:
+                    nc.sync.dma_start(out=out_words[0:64, 512 * side:512 * (side + 1)], in_=codes[0][rows].bitcast(I32))
+                else:
+                    nc.sync.dma_start(
+                        out=out_words[64:P].rearrange("p (h s c) -> p s h c", h=2, s=2)[:, side],
+                        in_=codes[1][rows].bitcast(I32).rearrange("p (h c) -> p h c", h=2))
+            for q in range(4):
+                side, jj = divmod(q, 2)
+                rows = slice(8 * jp + 4 * jj, 8 * jp + 4 * jj + 4)
+                src = planes[jp][32 * q:32 * q + 4].bitcast(I32)
+                if jp == 0:
+                    nc.sync.dma_start(out=out_scales[rows, 128 * side:128 * (side + 1)], in_=src)
+                else:
+                    nc.sync.dma_start(
+                        out=out_scales[rows].rearrange("b (h s c) -> b s h c", h=2, s=2)[:, side],
+                        in_=src.rearrange("b (h c) -> b h c", h=2))

from contextlib import ExitStack

import concourse.mybir as mybir
from concourse.masks import make_identity

K, T, E, C, H, PAD = 512, 1024, 8, 128, 512, 64
S = E * C
WIN = S + T + PAD
FLOPS = 3 * 2 * K * H * S

F32 = mybir.dt.float32
BF16 = mybir.dt.bfloat16
I32 = mybir.dt.int32
U32 = mybir.dt.uint32
U16 = mybir.dt.uint16
U8 = mybir.dt.uint8
FP8X4 = mybir.dt.float8_e4m3fn_x4
FP4X4 = mybir.dt.float4_e2m1fn_x4
ACT = mybir.ActivationFunctionType
ALU = mybir.AluOpType

P = 128
NB = T // P
GB = 5
KICKS = (0, 0, 0)
LATE_Y3 = False
W_LOADS = ((0, 2), (2, 3), (5, 3))
GROUPS = ((0, 2), (2, 2), (4, 2), (6, 1), (7, 1))


def tile_moe_cpy_glu_relu_kernel(
    tc, x_words, x_scales, xr, w1_words, w1_scales, w3_words, w3_scales, w2_words, w2_scales,
    gate, offs, pos1, pos2, out_0, out_1, out_2,
):
    nc = tc.nc
    with ExitStack() as ctx:
        keep = ctx.enter_context(tc.tile_pool(name="keep", bufs=1))
        ring = ctx.enter_context(tc.tile_pool(name="ring", bufs=2))
        psum = ctx.enter_context(tc.psum_pool(name="psum", bufs=1))

        def bank(b, shape, name):
            return psum.tile(shape, F32, name=name, tag="bank%d" % b)

        def held(shape, dtype, name):
            return keep.tile(shape, dtype, name=name, align_bytes=64)

        offs_t = keep.tile([P, S // 16], U16, name="offs_t")
        pos_t = [keep.tile([P, T // 16], U16, name="pos%d_t" % r) for r in (1, 2)]
        xw = held([P, T], I32, "xw")
        xs = held([P, T], U8, "xs")
        w1s = held([P, E * H], U8, "w1s")
        w3s = held([P, E * H], U8, "w3s")
        w2s = held([P, E * K], U8, "w2s")
        w1w = [held([P, n * 2 * H], U8, "w1w%d" % e0) for e0, n in W_LOADS]
        w3w = [held([P, n * 2 * H], U8, "w3w%d" % e0) for e0, n in W_LOADS]
        w2w = [held([P, E, 512], U8, "w2w%d" % jp) for jp in range(2)]
        win = [held([P, WIN], F32, "win%d" % j) for j in range(4)]
        ident = held([P, P], F32, "ident")
        grows = held([P, P], F32, "grows")
        gcol = held([P, 2 * NB], F32, "gcol")

        def load_scales(plane, src, n_e):
            view = src.rearrange("e s (q r) w -> r q (e s) w", r=4)
            dst = plane[:].rearrange("p (e w) -> p e w", e=n_e)
            for r in range(4):
                nc.sync.dma_start(out=dst[r:P:32].bitcast(I32), in_=view[r].bitcast(I32))

        def load_words(dst, src, i):
            e0, n = W_LOADS[i]
            view = src.rearrange("e s p c -> p (e s) c")[:, e0:e0 + n, :]
            nc.sync.dma_start(out=dst[i][:].rearrange("p (e c) -> p e c", e=n).bitcast(I32), in_=view.bitcast(I32))

        def expert_words(tiles, e):
            i = max(k for k, (e0, n) in enumerate(W_LOADS) if e0 <= e)
            u = e - W_LOADS[i][0]
            return tiles[i][:, u * 2 * H:(u + 1) * 2 * H]

        nc.gpsimd.memset(xs[:].bitcast(I32), 0)
        nc.vector.memset(w1s[:].bitcast(I32), 0)
        nc.vector.memset(w3s[:].bitcast(I32), 0)
        nc.gpsimd.memset(grows[:], 0.0)
        gate_rows = gate.rearrange("r a (b c) -> (r a b) c", c=P)
        nc.gpsimd.dma_start(out=grows[0:2 * NB, :], in_=gate_rows[(P - 1) * NB:(P + 1) * NB, :])
        make_identity(nc, ident[:])
        nc.gpsimd.memset(w2s[:].bitcast(I32), 0)
        for j in range(4):
            nc.gpsimd.memset(win[j][:, S + T:], 0.0)

        nc.sync.dma_start(offs_t[:], offs)
        xs_view = x_scales.rearrange("s (q r) t -> r q (s t)", r=4)
        for r in range(4):
            if r == 3:
                nc.sync.dma_start(out=xw[:], in_=x_words.rearrange("s p t d -> p (s t d)").bitcast(I32))
            nc.sync.dma_start(out=xs[r:P:32, :].bitcast(I32), in_=xs_view[r].bitcast(I32))
        load_words(w1w, w1_words, 0)
        load_words(w3w, w3_words, 0)
        load_scales(w1s, w1_scales, E)
        load_scales(w3s, w3_scales, E)
        for i in (1, 2):
            load_words(w1w, w1_words, i)
            load_words(w3w, w3_words, i)
        load_scales(w2s, w2_scales, E)
        w2_view = w2_words.rearrange("e s p c -> p (e s) c")
        def load_w2(jp):
            nc.sync.dma_start(out=w2w[jp][:].bitcast(I32), in_=w2_view[:, :, 512 * jp:512 * (jp + 1)].bitcast(I32))

        def load_xr(j):
            nc.sync.dma_start(out=win[j][:, S:S + T], in_=xr[j * P:(j + 1) * P, :])

        load_w2(0)
        load_xr(0)
        load_xr(1)
        load_w2(1)
        nc.sync.dma_start(pos_t[0][:], pos1)
        load_xr(2)
        load_xr(3)
        nc.sync.dma_start(pos_t[1][:], pos2)

        gps = bank(7, [P, P], "gps")
        nc.tensor.transpose(gps[:], grows[:], ident[:])
        nc.scalar.activation(gcol[:], gps[:, 0:2 * NB], ACT.Copy)

        xg, xgs = [], []

        for hf in range(2):
            gw = held([P, 4 * C], I32, "xg%d" % hf)
            gs = held([P, 4 * C], U8, "xgs%d" % hf)
            sl = offs_t[:, hf * 32:(hf + 1) * 32]
            nc.vector.tensor_copy(gw[:].bitcast(U32), xw[:].bitcast(U32).indirect(sl))
            nc.vector.tensor_copy(gs[:], xs[:].indirect(sl))
            xg.append(gw)
            xgs.append(gs)

        hq, hqs = {}, {}

        def w2_cols(e, j):
            return w2w[j // 2][:, e, (j % 2) * 256:(j % 2 + 1) * 256]

        def second_layer(dst, j, e):
            nc.tensor.matmul_mx(
                out=dst, lhsT=w2_cols(e, j).bitcast(FP4X4),
                lhsT_scale=w2s[:, e * K + j * P:e * K + (j + 1) * P],
                rhs=hq[e].bitcast(FP8X4), rhs_scale=hqs[e], start=True, stop=True,
            )

        hb = {}

        def first_layer(e):
            pr, u = divmod(e, 4)
            tok = xg[pr][:, u * C:(u + 1) * C].bitcast(FP8X4)
            tok_s = xgs[pr][:, u * C:(u + 1) * C]
            a = bank((0, 1, 2, 5)[e % 4], [P, H], "a")
            b = bank((3, 4, 6, 7)[e % 4], [P, H], "b")
            for dst, ww, ws in ((a, w1w, w1s), (b, w3w, w3s)):
                nc.tensor.matmul_mx(
                    out=dst[:], lhsT=tok, lhsT_scale=tok_s,
                    rhs=expert_words(ww, e).bitcast(FP4X4),
                    rhs_scale=ws[:, e * H:(e + 1) * H], start=True, stop=True,
                )
            ra = ring.tile([P, H], F32, name="ra", bufs=4)
            nc.scalar.activation(
                ra[:].rearrange("s (u p w) -> s u p w", u=2, w=2),
                a[:].rearrange("s (p u w) -> s u p w", u=2, w=2), ACT.Relu)
            h = ring.tile([P, H], BF16, name="h", bufs=8, align_bytes=64)
            nc.vector.tensor_tensor(
                h[:].rearrange("s (u p w) -> s u p w", u=2, w=2),
                b[:].rearrange("s (p u w) -> s u p w", u=2, w=2),
                ra[:].rearrange("s (u p w) -> s u p w", u=2, w=2), ALU.mult)
            hb[e] = h

        def turn_and_quantise(gi, bk):
            e0, n = GROUPS[gi]
            ht = bank(bk, [P, n, 2, C], "ht")
            for u in range(n):
                words = hb[e0 + u][:].bitcast(F32)
                for v in range(2):
                    nc.tensor.transpose(ht[:, u, v, :], words[:, v * P:(v + 1) * P], ident[:])
            hin = ring.tile([P, n * H], BF16, name="hin", bufs=3, align_bytes=64)
            copy = nc.scalar.copy if gi < 2 else nc.vector.tensor_copy
            copy(
                hin[:].bitcast(F32).rearrange("p (u s v) -> p u s v", u=n, v=2),
                ht[:].rearrange("p u v s -> p u s v"))
            q = held([P, n * C], U32, "hq%d" % gi)
            qs = held([P, n * C], U8, "hqs%d" % gi)
            nc.vector.quantize_mx(out=q[:].bitcast(FP8X4), scales=qs[:], in_=hin[:])
            for u in range(n):
                hq[e0 + u] = q[:, u * C:(u + 1) * C]
                hqs[e0 + u] = qs[:, u * C:(u + 1) * C]

        def slots_out(j, e0, n, bk):
            yb = bank(bk, [P, n * C], "y")
            for u in range(n):
                second_layer(yb[:, u * C:(u + 1) * C], j, e0 + u)
            nc.scalar.copy(win[j][:, e0 * C:(e0 + n) * C], yb[:])

        for e in range(E):
            first_layer(e)
        for gi, bk in enumerate((0, 1, 2, 5, 3)):
            turn_and_quantise(gi, bk)
        slots_out(0, 0, 4, 4)
        slots_out(0, 4, 3, 6)
        slots_out(0, 7, 1, 7)
        slots_out(1, 0, 4, 0)
        slots_out(1, 4, 3, 1)
        slots_out(1, 7, 1, 2)
        A, B, Cb, D, Eb, Fb, G, Hb = 0, 1, 2, 5, 3, 4, 6, 7
        def row_block(j, banks):
            for hf in range(2):
                slots_out(j, 4 * hf, 4, banks[hf])

        def kick(n, bk):
            if n:
                spare = bank(bk, [P, H], "spare")
            for i in range(n):
                nc.tensor.matmul_mx(
                    out=spare[:], lhsT=xg[0][:, 0:C].bitcast(FP8X4), lhsT_scale=xgs[0][:, 0:C],
                    rhs=expert_words(w1w, 0).bitcast(FP4X4), rhs_scale=w1s[:, 0:H], start=True, stop=True)

        row_block(2, (D, Cb))
        if not LATE_Y3:
            row_block(3, (Eb, Fb))

        def place(jp, tb):
            if jp == 0:
                return tb % 4, tb // 4
            return 2 * (tb // 4) + tb % 2, (tb % 4) // 2

        sc = [[[held([P, 4, P], F32, "sc%d_%d_%d" % (r, jp, u)) for u in range(4)] for jp in range(2)]
              for r in range(2)]
        back = {}

        def fetch(r, j, tb0, order, banks):
            jp, jj = divmod(j, 2)
            ntb = len(order)
            g = ring.tile([P, ntb * P], F32, name="g", bufs=GB)
            nc.vector.tensor_copy(g[:], win[j][:].indirect(pos_t[r][:, tb0 * 8:(tb0 + ntb) * 8]))
            for k, bk in enumerate(banks):
                fb = bank(bk, [P, 4, P], "fwd")
                tbs = order[4 * k:4 * k + 4]
                for i, tb in enumerate(tbs):
                    nc.tensor.transpose(fb[:, i, :], g[:, (tb - tb0) * P:(tb - tb0 + 1) * P], ident[:])
                for i, tb in enumerate(tbs):
                    u, side = place(jp, tb)
                    nc.scalar.activation(
                        sc[r][jp][u][:, :, 64 * side + 32 * jj:64 * side + 32 * (jj + 1)],
                        fb[:, i, :].rearrange("c (p d) -> c d p", d=4),
                        ACT.Copy, scale=gcol[:, r * NB + tb:r * NB + tb + 1])

        def turn_back(r, jp, u, bk):
            if r == 0:
                back[u] = bank(bk, [P, 4, P], "back")
            for d in range(4):
                nc.tensor.matmul(back[u][:, d, :], sc[r][jp][u][:, d, :], ident[:], is_transpose=True,
                                 start=(r == 0 and d == 0), stop=(r == 1 and d == 3))

        out_rows = out_0.rearrange("(p d) t -> p d t", d=4)
        out_words = out_1.rearrange("s p t d -> p (s t d)").bitcast(I32)
        out_scales = out_2.rearrange("s b t -> b (s t)").bitcast(I32)
        osb0 = held([P, 4, 4 * P], F32, "osb0")
        osb1 = [held([P, 4, 2 * P], F32, "osb1_%d" % h) for h in range(2)]
        codes = [held([P, 4 * P], U32, "codes%d" % jp) for jp in range(2)]
        planes = [held([P, 4 * P], U8, "planes%d" % jp) for jp in range(2)]

        def sums(jp, u):
            if jp == 0:
                return osb0[:, :, u * P:(u + 1) * P]
            return osb1[u // 2][:, :, (u % 2) * P:(u % 2 + 1) * P]

        def round_out(jp, u0, n, src):
            rb = rounded[:, (4 * jp + u0) * 4 * P:(4 * jp + u0 + n) * 4 * P]
            nc.vector.tensor_copy(rb.rearrange("p (c d) -> p c d", d=4), src.rearrange("p d c -> p c d"))

        def quantise_out(jp, u0, n):
            rb = rounded[:, (4 * jp + u0) * 4 * P:(4 * jp + u0 + n) * 4 * P]
            cols = slice(u0 * P, (u0 + n) * P)
            nc.vector.quantize_mx(out=codes[jp][:, cols].bitcast(FP8X4), scales=planes[jp][:, cols], in_=rb)

        order0 = (0, 4, 1, 5, 2, 6, 3, 7)
        order1 = (0, 2, 1, 3, 4, 6, 5, 7)
        fetch(0, 0, 0, order0, (G, Hb))
        fetch(0, 1, 0, order0, (A, B))
        turn_back(0, 0, 0, Cb)
        turn_back(0, 0, 1, D)
        fetch(1, 0, 0, order0, (A, B))
        turn_back(0, 0, 2, Eb)
        turn_back(0, 0, 3, Fb)
        fetch(1, 1, 0, order0, (A, B))
        for u in range(4):
            if u == 2:
                fetch(0, 2, 0, order1, (A, B))
            turn_back(1, 0, u, None)
            nc.scalar.copy(sums(0, u), back[u][:])
        for side in range(2):
            nc.sync.dma_start(out=out_rows[0:64, :, 512 * side:512 * (side + 1)], in_=osb0[64 * side:64 * (side + 1)])
        fetch(0, 3, 0, order1, (Cb, D))
        fetch(1, 2, 0, order1[0:4], (A,))
        fetch(1, 3, 0, order1[0:4], (B,))
        turn_back(0, 1, 0, G)
        turn_back(0, 1, 1, Hb)
        fetch(1, 2, 4, order1[4:8], (Cb,))
        turn_back(0, 1, 2, Eb)
        turn_back(0, 1, 3, Fb)
        fetch(1, 3, 4, order1[4:8], (D,))
        for u in range(4):
            turn_back(1, 1, u, None)
        rounded = keep.tile([P, 8 * 4 * P], BF16, name="rounded", tag="win3", align_bytes=64)
        for h in range(2):
            for u in (2 * h, 2 * h + 1):
                nc.scalar.copy(sums(1, u), back[u][:])
            for side in range(2):
                first = 512 * h + 256 * side
                nc.sync.dma_start(out=out_rows[64:P, :, first:first + 256], in_=osb1[h][64 * side:64 * (side + 1)])
        for jp in range(2):
            if jp == 0:
                round_out(0, 0, 4, osb0[:])
                quantise_out(0, 0, 4)
            else:
                round_out(1, 0, 2, osb1[0][:])
                round_out(1, 2, 1, sums(1, 2))
                quantise_out(1, 0, 2)
                round_out(1, 3, 1, sums(1, 3))
                quantise_out(1, 2, 1)
                quantise_out(1, 3, 1)
            for side in range(2):
                rows = slice(64 * side, 64 * (side + 1))
                if jp == 0:
                    nc.sync.dma_start(out=out_words[0:64, 512 * side:512 * (side + 1)], in_=codes[0][rows].bitcast(I32))
                else:
                    nc.sync.dma_start(
                        out=out_words[64:P].rearrange("p (h s c) -> p s h c", h=2, s=2)[:, side],
                        in_=codes[1][rows].bitcast(I32).rearrange("p (h c) -> p h c", h=2))
            for q in range(4):
                side, jj = divmod(q, 2)
                rows = slice(8 * jp + 4 * jj, 8 * jp + 4 * jj + 4)
                src = planes[jp][32 * q:32 * q + 4].bitcast(I32)
                if jp == 0:
                    nc.sync.dma_start(out=out_scales[rows, 128 * side:128 * (side + 1)], in_=src)
                else:
                    nc.sync.dma_start(
                        out=out_scales[rows].rearrange("b (h s c) -> b s h c", h=2, s=2)[:, side],
                        in_=src.rearrange("b (h c) -> b h c", h=2))
